import numpy as np
import ml_dtypes


def mxq(x, axis, fmt="e4m3"):
    dtype, down = {"e4m3": (ml_dtypes.float8_e4m3fn, 7), "e5m2": (ml_dtypes.float8_e5m2, 14)}[fmt]
    v = np.moveaxis(np.asarray(x, np.float32).astype(ml_dtypes.bfloat16).astype(np.float64), axis, -1)
    blocks = v.reshape(v.shape[:-1] + (-1, 32))
    amax = np.abs(blocks).max(-1, keepdims=True)
    byte = np.maximum(np.where(amax > 0, np.frexp(amax)[1] - 1 + 127, 0) - down, 1)
    scale = np.exp2(byte - 127.0)
    codes = (blocks / scale).astype(np.float32).astype(dtype).astype(np.float64)
    return np.moveaxis((codes * scale).reshape(v.shape), -1, axis)


WIDE = False


def mx_kscale(k):
    if not WIDE:
        return np.ones(k)
    levels = np.array([30, -30])
    if k % 512:
        return np.exp2(np.random.permutation(np.resize(levels, k // 32))).repeat(32)
    a = np.empty((k // 512, 16))
    for p in range(k // 512):
        a[p, :8] = np.random.permutation(np.resize(levels, 8))
        for g in range(8):
            far = levels[np.abs(levels - a[p, g]) >= 10]
            a[p, g + 8] = far[np.random.randint(len(far))]
    return np.exp2(a.ravel()).repeat(32)


def f64(x):
    return np.asarray(x).astype(np.float64)


def striped(idx):
    return np.tile(np.asarray(idx).reshape(-1, 16).T, (8, 1)).astype(np.uint16)


def unstriped(offs):
    return offs[:16].T.reshape(-1).astype(np.int64)


E2M1 = np.array([0.0, 0.5, 1.0, 1.5, 2.0, 3.0, 4.0, 6.0, -0.0, -0.5, -1.0, -1.5, -2.0, -3.0, -4.0, -6.0])


def pack_weight(w, fmt):
    k, n = w.shape
    w = f64(np.asarray(w, np.float32).astype(ml_dtypes.bfloat16)).reshape(k // 32, 32, n)
    amax = np.abs(w).max(1)
    if fmt == "e4m3":
        byte = np.frexp(amax)[1] - 1 + 127 - 7
    else:
        mant, ex = np.frexp(amax / 6.0)
        byte = np.where(mant > 0.5, ex, ex - 1) + 127
    byte = np.clip(np.where(amax > 0, byte, 1), 1, 254)
    scaled = (w * np.exp2(127.0 - byte)[:, None, :]).reshape(k, n).astype(np.float32)
    by_word = np.ascontiguousarray(scaled.reshape(k // 512, 128, 4, n).transpose(0, 1, 3, 2))
    if fmt == "e4m3":
        words = by_word.astype(ml_dtypes.float8_e4m3fn).view(np.uint8)
    else:
        c = by_word.astype(ml_dtypes.float4_e2m1fn).view(np.uint8) & 0xF
        words = (c[..., 0::2] | (c[..., 1::2] << 4)).reshape(k // 512, 128, 2 * n)
    return np.ascontiguousarray(words), np.ascontiguousarray(byte.astype(np.uint8).reshape(k // 512, 16, n))


def unpack_weight(words, scales, fmt):
    g, _, n = scales.shape
    words = np.ascontiguousarray(words).reshape(g, 128, n, -1)
    if fmt == "e4m3":
        vals = words.view(ml_dtypes.float8_e4m3fn).astype(np.float64)
    else:
        nib = np.empty((g, 128, n, 4), np.uint8)
        nib[..., 0::2] = words & 0xF
        nib[..., 1::2] = words >> 4
        vals = E2M1[nib]
    vals = vals * np.repeat(np.exp2(scales.astype(np.float64) - 127.0), 8, axis=1)[..., None]
    return vals.transpose(0, 1, 3, 2).reshape(g * 512, n)


K, T, J, S, R, N = 512, 512, 256, 512, 512, 256


def setup_inputs():
    n = np.random.standard_normal
    idx = np.random.permutation(T)[:J]
    idx2 = np.random.permutation(S)[:J]
    fk = mx_kscale(K)
    fr = mx_kscale(R)
    wp = pack_weight(n((K, R)) * 1 / np.sqrt(K) * fk[:, None], "e2m1")
    wbp = pack_weight(n((R, N)) * 1 / np.sqrt(R) / fr[:, None], "e4m3")
    return {
        "xa": (n((K, T))).astype(np.float32),
        "xb": (n((K, S))).astype(np.float32),
        "fk": (np.random.uniform(0.5, 2.0, (K, 1)) / fk[:, None]).astype(np.float32),
        "w_words": wp[0],
        "w_scales": wp[1],
        "us": (np.random.uniform(0.5, 1.5, (1, R)) * fr).astype(np.float32),
        "wb_words": wbp[0],
        "wb_scales": wbp[1],
        "rs": (n((N, J))).astype(np.float32),
        "gm": (np.random.uniform(0.5, 2.0, (N, 1))).astype(np.float32),
        "offs": striped(idx),
        "offs2": striped(idx2),
    }


def reference(xa, xb, fk, w_words, w_scales, us, wb_words, wb_scales, rs, gm, offs, offs2):
    idx = unstriped(offs)
    idx2 = unstriped(offs2)
    wu = unpack_weight(w_words, w_scales, "e2m1")
    wbu = unpack_weight(wb_words, wb_scales, "e4m3")
    u = f64(xa)[:, idx] * f64(xb)[:, idx2] * f64(fk)
    uq = mxq(u, 0, "e4m3")
    a = uq.T @ wu
    m1 = np.max(a, axis=1, keepdims=True)
    hr = np.maximum(a, 0.0) / (m1 + 0.3) * f64(us)
    hid = hr.T
    hidq = mxq(hid, 0, "e5m2")
    p = wbu.T @ hidq
    y = f64(gm) * p + f64(rs)
    return y

@@ -1,0 +1,160 @@
+from contextlib import ExitStack
+
+import concourse.mybir as mybir
+
+K, T, J, S, R, N = 512, 512, 256, 512, 512, 256
+FLOPS = 2 * K * J * R + 2 * R * N * J
+
+F32 = mybir.dt.float32
+BF16 = mybir.dt.bfloat16
+I32 = mybir.dt.int32
+U32 = mybir.dt.uint32
+U16 = mybir.dt.uint16
+U8 = mybir.dt.uint8
+E4M3X4 = mybir.dt.float8_e4m3fn_x4
+E5M2X4 = mybir.dt.float8_e5m2_x4
+E2M1X4 = mybir.dt.float4_e2m1fn_x4
+ALU = mybir.AluOpType
+ACT = mybir.ActivationFunctionType
+
+P = 128
+PACK = 4
+HALVES = J // P
+LIST_COLS = P // 16
+PEAK_SHIFT = 0.3
+
+
+def load_scale_rows(queue, plane, scales):
+    for q in range(4):
+        queue.dma_start(out=plane[32 * q : 32 * q + 4, :].bitcast(I32), in_=scales[0, 4 * q : 4 * q + 4, :].bitcast(I32))
+
+
+def tile_list_rows_entryproducts_peak_residual_kernel(
+    tc, xa, xb, fk, w_words, w_scales, us, wb_words, wb_scales, rs, gm, offs, offs2, out
+):
+    nc = tc.nc
+    with ExitStack() as ctx:
+        lists = ctx.enter_context(tc.tile_pool(name="lists", bufs=1))
+        sb = ctx.enter_context(tc.tile_pool(name="sb", bufs=1))
+        ps = ctx.enter_context(tc.psum_pool(name="ps", bufs=1))
+
+        list_a = lists.tile([P, J // 16], U16, name="list_a")
+        list_b = lists.tile([P, J // 16], U16, name="list_b")
+        xa_rows = xa.rearrange("(p t) c -> t p c", t=PACK)
+        xb_rows = xb.rearrange("(p t) c -> t p c", t=PACK)
+        xa_sb = [sb.tile([P, T], F32, name=f"xa{t}") for t in range(PACK)]
+        xb_sb = [sb.tile([P, S], F32, name=f"xb{t}") for t in range(PACK)]
+        fk_sb = sb.tile([P, PACK], F32, name="fk_sb")
+        us_sb = sb.tile([P, PACK], F32, name="us_sb")
+        gm_sb = sb.tile([P, N // P], F32, name="gm_sb")
+        rs_sb = sb.tile([P, N // P, J], F32, name="rs_sb")
+        w_sb = sb.tile([P, 2 * R], U8, name="w_sb", align_bytes=64)
+        w_sc = sb.tile([P, R], U8, name="w_sc", align_bytes=64)
+        wb_sb = sb.tile([P, N], U32, name="wb_sb", align_bytes=64)
+        wb_sc = sb.tile([P, N], U8, name="wb_sc", align_bytes=64)
+
+        nc.sync.dma_start(out=xa_sb[0][:], in_=xa_rows[0])
+        nc.sync.dma_start(list_a[:], offs)
+        nc.scalar.dma_start(out=fk_sb[:], in_=fk.rearrange("(p t) o -> p (t o)", t=PACK))
+        nc.scalar.dma_start(out=us_sb[:], in_=us.rearrange("o (p t) -> p (o t)", t=PACK))
+        nc.sync.dma_start(out=xa_sb[1][:], in_=xa_rows[1])
+        nc.sync.dma_start(list_b[:], offs2)
+        for t in range(PACK):
+            nc.sync.dma_start(out=xb_sb[t][:], in_=xb_rows[t])
+            if t + 2 < PACK:
+                nc.sync.dma_start(out=xa_sb[t + 2][:], in_=xa_rows[t + 2])
+        load_scale_rows(nc.sync, w_sc, w_scales)
+        nc.sync.dma_start(out=w_sb[:].bitcast(I32), in_=w_words[0].bitcast(I32))
+        load_scale_rows(nc.sync, wb_sc, wb_scales)
+        nc.sync.dma_start(out=wb_sb[:].bitcast(I32), in_=wb_words[0].rearrange("p n t -> p (n t)").bitcast(I32))
+        nc.sync.dma_start(out=rs_sb[:], in_=rs.rearrange("(c p) j -> p c j", p=P))
+        with nc.allow_non_contiguous_dma(reason="one factor a partition"):
+            nc.sync.dma_start(out=gm_sb[:], in_=gm.rearrange("(c p) o -> p (c o)", p=P))
+
+        ident = sb.tile([P, P], F32, name="ident")
+        offset = sb.tile([P, P], F32, name="offset")
+        distance = sb.tile([P, P], F32, name="distance", tag="picked0")
+        nc.gpsimd.iota(offset[:], pattern=[[1, P]], base=0, channel_multiplier=-1, allow_small_or_imprecise_dtypes=True)
+        nc.scalar.activation(out=distance[:], in_=offset[:], func=ACT.Abs)
+        nc.scalar.activation(out=ident[:], in_=distance[:], func=ACT.Relu, scale=-1.0, bias=1.0)
+
+        us_all = ps.tile([P, 2, P, 2], F32, name="us_all")
+        for t in range(PACK):
+            nc.tensor.transpose(us_all[:, t // 2, :, t % 2], us_sb[:, t : t + 1].to_broadcast([P, P]), ident[:])
+
+        picked = [sb.tile([P, J], F32, name=f"picked{t}", tag=f"picked{t}") for t in range(PACK)]
+        scaled = [sb.tile([P, J], F32, name=f"scaled{t}") for t in range(PACK)]
+        for t in range(PACK):
+            nc.scalar.activation(out=picked[t][:], in_=xa_sb[t][:].indirect(list_a[:]), func=ACT.Copy)
+            nc.scalar.activation(out=scaled[t][:], in_=picked[t][:], func=ACT.Copy, scale=fk_sb[:, t : t + 1])
+
+        u_bf = [sb.tile([P, P, PACK], BF16, name=f"u_bf{h}", align_bytes=64) for h in range(HALVES)]
+        prod_lo = sb.tile([P, 2, J], F32, name="prod_lo")
+        prod_hi = [sb.tile([P, 2, P], F32, name=f"prod_hi{h}") for h in range(HALVES)]
+        for t in range(2):
+            nc.vector.tensor_tensor(prod_lo[:, t, :], xb_sb[t][:].indirect(list_b[:]), scaled[t][:], ALU.mult)
+        for h in range(HALVES):
+            nc.vector.tensor_copy(out=u_bf[h][:, :, 0:2], in_=prod_lo[:, :, h * P : (h + 1) * P].rearrange("p t j -> p j t"))
+        for t in range(2, PACK):
+            for h in range(HALVES):
+                nc.vector.tensor_tensor(
+                    prod_hi[h][:, t - 2, :],
+                    xb_sb[t][:].indirect(list_b[:, h * LIST_COLS : (h + 1) * LIST_COLS]),
+                    scaled[t][:, h * P : (h + 1) * P],
+                    ALU.mult,
+                )
+        for h in range(HALVES):
+            nc.vector.tensor_copy(out=u_bf[h][:, :, 2:4], in_=prod_hi[h][:].rearrange("p t j -> p j t"))
+        u_q = [sb.tile([P, P], U32, name=f"u_q{h}", align_bytes=64) for h in range(HALVES)]
+        u_sc = [sb.tile([P, P], U8, name=f"u_sc{h}", align_bytes=64) for h in range(HALVES)]
+        a_ps = [ps.tile([P, R], F32, name=f"a_ps{h}") for h in range(HALVES)]
+        for h in range(HALVES):
+            nc.vector.quantize_mx(out=u_q[h][:].bitcast(E4M3X4), scales=u_sc[h][:], in_=u_bf[h][:].rearrange("p j t -> p (j t)"))
+            nc.tensor.matmul_mx(
+                out=a_ps[h][:], lhsT=u_q[h][:].bitcast(E4M3X4), lhsT_scale=u_sc[h][:],
+                rhs=w_sb[:].bitcast(E2M1X4), rhs_scale=w_sc[:], start=True, stop=True,
+            )
+
+        pos = [sb.tile([P, 2, P, 2], F32, name=f"pos{h}") for h in range(HALVES)]
+        peak = [sb.tile([P, 1], F32, name=f"peak{h}") for h in range(HALVES)]
+        den = [sb.tile([P, 1], F32, name=f"den{h}") for h in range(HALVES)]
+        inv = [sb.tile([P, 1], F32, name=f"inv{h}") for h in range(HALVES)]
+        hr = [sb.tile([P, R], BF16, name=f"hr{h}") for h in range(HALVES)]
+        for h in range(HALVES):
+            nc.vector.tensor_scalar(
+                out=pos[h][:], in0=a_ps[h][:].rearrange("p (q u e) -> p u q e", u=2, e=2),
+                scalar1=0.0, scalar2=None, op0=ALU.max, op1=ALU.max, accum_out=peak[h][:],
+            )
+            nc.vector.tensor_scalar(out=den[h][:], in0=peak[h][:], scalar1=PEAK_SHIFT, scalar2=None, op0=ALU.add)
+            nc.vector.reciprocal(out=inv[h][:], in_=den[h][:])
+        t_ps = [ps.tile([P, 2, P], F32, name=f"t_ps{h}") for h in range(HALVES)]
+        hid_bf = [sb.tile([P, P, PACK], BF16, name=f"hid_bf{h}", align_bytes=64) for h in range(HALVES)]
+        for h in range(HALVES):
+            nc.vector.scalar_tensor_tensor(
+                out=hr[h][:], in0=pos[h][:].rearrange("p u q e -> p (u q e)"), scalar=inv[h][:],
+                in1=us_all[:].rearrange("p u q e -> p (u q e)"), op0=ALU.mult, op1=ALU.mult,
+            )
+            words = hr[h][:].bitcast(F32)
+            for u in range(2):
+                nc.tensor.transpose(t_ps[h][:, u, :], words[:, u * P : (u + 1) * P], ident[:])
+            nc.scalar.copy(out=hid_bf[h][:].bitcast(F32), in_=t_ps[h][:].rearrange("p u j -> p j u"))
+
+        hid_q = [sb.tile([P, P], U32, name=f"hid_q{h}", align_bytes=64) for h in range(HALVES)]
+        hid_sc = [sb.tile([P, P], U8, name=f"hid_sc{h}", align_bytes=64) for h in range(HALVES)]
+        p_ps = [ps.tile([P, N // P, P], F32, name=f"p_ps{h}") for h in range(HALVES)]
+        res = [sb.tile([P, N // P, P], F32, name=f"res{h}") for h in range(HALVES)]
+        out_rows = out.rearrange("(c p) j -> p c j", p=P)
+        for h in range(HALVES):
+            nc.vector.quantize_mx(out=hid_q[h][:].bitcast(E5M2X4), scales=hid_sc[h][:], in_=hid_bf[h][:].rearrange("p j t -> p (j t)"))
+            for c in range(N // P):
+                nc.tensor.matmul_mx(
+                    out=p_ps[h][:, c, :], lhsT=wb_sb[:, c * P : (c + 1) * P].bitcast(E4M3X4), lhsT_scale=wb_sc[:, c * P : (c + 1) * P],
+                    rhs=hid_q[h][:].bitcast(E5M2X4), rhs_scale=hid_sc[h][:], start=True, stop=True,
+                )
+        for h in range(HALVES):
+            for c in range(N // P):
+                nc.vector.scalar_tensor_tensor(
+                    out=res[h][:, c, :], in0=p_ps[h][:, c, :], scalar=gm_sb[:, c : c + 1],
+                    in1=rs_sb[:, c, h * P : (h + 1) * P], op0=ALU.mult, op1=ALU.add,
+                )
+            nc.sync.dma_start(out=out_rows[:, :, h * P : (h + 1) * P], in_=res[h][:])

@@ -42,7 +42,9 @@ def tile_list_rows_entryproducts_peak_residual_kernel(
         list_b = lists.tile([P, J // 16], U16, name="list_b")
         xa_rows = xa.rearrange("(p t) c -> t p c", t=PACK)
         xb_rows = xb.rearrange("(p t) c -> t p c", t=PACK)
-        xa_sb = [sb.tile([P, T], F32, name=f"xa{t}") for t in range(PACK)]
+        xa_lo = [sb.tile([P, T], F32, name=f"xa{t}") for t in range(2)]
+        xa_hi = sb.tile([P, 2, T], F32, name="xa_hi")
+        xa_sb = [xa_lo[0][:], xa_lo[1][:], xa_hi[:, 0, :], xa_hi[:, 1, :]]
         xb_sb = [sb.tile([P, S], F32, name=f"xb{t}") for t in range(PACK)]
         fk_sb = sb.tile([P, PACK], F32, name="fk_sb")
         us_sb = sb.tile([P, PACK], F32, name="us_sb")
@@ -53,18 +55,18 @@ def tile_list_rows_entryproducts_peak_residual_kernel(
         wb_sb = sb.tile([P, N], U32, name="wb_sb", align_bytes=64)
         wb_sc = sb.tile([P, N], U8, name="wb_sc", align_bytes=64)
 
-        nc.sync.dma_start(out=xa_sb[0][:], in_=xa_rows[0])
         nc.sync.dma_start(list_a[:], offs)
-        nc.scalar.dma_start(out=fk_sb[:], in_=fk.rearrange("(p t) o -> p (t o)", t=PACK))
-        nc.scalar.dma_start(out=us_sb[:], in_=us.rearrange("o (p t) -> p (o t)", t=PACK))
-        nc.sync.dma_start(out=xa_sb[1][:], in_=xa_rows[1])
+        nc.sync.dma_start(out=xa_sb[0], in_=xa_rows[0])
+        nc.sync.dma_start(out=fk_sb[:], in_=fk.rearrange("(p t) o -> p (t o)", t=PACK))
+        nc.sync.dma_start(out=xa_sb[1], in_=xa_rows[1])
+        nc.sync.dma_start(out=xa_hi[:], in_=xa.rearrange("(p t) c -> p t c", t=PACK)[:, 2:4, :])
         nc.sync.dma_start(list_b[:], offs2)
-        for t in range(PACK):
+        nc.sync.dma_start(out=xb_sb[0][:], in_=xb_rows[0])
+        nc.sync.dma_start(out=us_sb[:], in_=us.rearrange("o (p t) -> p (o t)", t=PACK))
+        for t in range(1, PACK):
             nc.sync.dma_start(out=xb_sb[t][:], in_=xb_rows[t])
-            if t + 2 < PACK:
-                nc.sync.dma_start(out=xa_sb[t + 2][:], in_=xa_rows[t + 2])
-        load_scale_rows(nc.sync, w_sc, w_scales)
         nc.sync.dma_start(out=w_sb[:].bitcast(I32), in_=w_words[0].bitcast(I32))
+        load_scale_rows(nc.sync, w_sc, w_scales)
         load_scale_rows(nc.sync, wb_sc, wb_scales)
         nc.sync.dma_start(out=wb_sb[:].bitcast(I32), in_=wb_words[0].rearrange("p n t -> p (n t)").bitcast(I32))
         nc.sync.dma_start(out=rs_sb[:], in_=rs.rearrange("(c p) j -> p c j", p=P))
@@ -72,8 +74,8 @@ def tile_list_rows_entryproducts_peak_residual_kernel(
             nc.sync.dma_start(out=gm_sb[:], in_=gm.rearrange("(c p) o -> p (c o)", p=P))
 
         ident = sb.tile([P, P], F32, name="ident")
-        offset = sb.tile([P, P], F32, name="offset")
-        distance = sb.tile([P, P], F32, name="distance", tag="picked0")
+        offset = sb.tile([P, P], F32, name="offset", tag="picked_lo")
+        distance = sb.tile([P, P], F32, name="distance", tag="picked_hi")
         nc.gpsimd.iota(offset[:], pattern=[[1, P]], base=0, channel_multiplier=-1, allow_small_or_imprecise_dtypes=True)
         nc.scalar.activation(out=distance[:], in_=offset[:], func=ACT.Abs)
         nc.scalar.activation(out=ident[:], in_=distance[:], func=ACT.Relu, scale=-1.0, bias=1.0)
@@ -82,67 +84,78 @@ def tile_list_rows_entryproducts_peak_residual_kernel(
         for t in range(PACK):
             nc.tensor.transpose(us_all[:, t // 2, :, t % 2], us_sb[:, t : t + 1].to_broadcast([P, P]), ident[:])
 
-        picked = [sb.tile([P, J], F32, name=f"picked{t}", tag=f"picked{t}") for t in range(PACK)]
+        picked_lo = sb.tile([P, 2, J], F32, name="picked_lo", tag="picked_lo")
+        picked_hi = sb.tile([P, 2, J], F32, name="picked_hi", tag="picked_hi")
+        picked = [picked_lo[:, 0, :], picked_lo[:, 1, :], picked_hi[:, 0, :], picked_hi[:, 1, :]]
         scaled = [sb.tile([P, J], F32, name=f"scaled{t}") for t in range(PACK)]
         for t in range(PACK):
-            nc.scalar.activation(out=picked[t][:], in_=xa_sb[t][:].indirect(list_a[:]), func=ACT.Copy)
-            nc.scalar.activation(out=scaled[t][:], in_=picked[t][:], func=ACT.Copy, scale=fk_sb[:, t : t + 1])
+            nc.scalar.activation(out=picked[t], in_=xa_sb[t].indirect(list_a[:]), func=ACT.Copy)
+        for t in range(2):
+            nc.vector.tensor_scalar(out=scaled[t][:], in0=picked[t], scalar1=fk_sb[:, t : t + 1], scalar2=None, op0=ALU.mult)
+        for t in range(2, PACK):
+            nc.scalar.activation(out=scaled[t][:], in_=picked[t], func=ACT.Copy, scale=fk_sb[:, t : t + 1])
 
         u_bf = [sb.tile([P, P, PACK], BF16, name=f"u_bf{h}", align_bytes=64) for h in range(HALVES)]
-        prod_lo = sb.tile([P, 2, J], F32, name="prod_lo")
-        prod_hi = [sb.tile([P, 2, P], F32, name=f"prod_hi{h}") for h in range(HALVES)]
+        prod_lo = sb.tile([P, 2, J], F32, name="prod_lo", tag="picked_lo")
+        prod_hi = sb.tile([P, 2, J], F32, name="prod_hi")
         for t in range(2):
             nc.vector.tensor_tensor(prod_lo[:, t, :], xb_sb[t][:].indirect(list_b[:]), scaled[t][:], ALU.mult)
         for h in range(HALVES):
-            nc.vector.tensor_copy(out=u_bf[h][:, :, 0:2], in_=prod_lo[:, :, h * P : (h + 1) * P].rearrange("p t j -> p j t"))
-        for t in range(2, PACK):
-            for h in range(HALVES):
-                nc.vector.tensor_tensor(
-                    prod_hi[h][:, t - 2, :],
-                    xb_sb[t][:].indirect(list_b[:, h * LIST_COLS : (h + 1) * LIST_COLS]),
-                    scaled[t][:, h * P : (h + 1) * P],
-                    ALU.mult,
-                )
+            nc.scalar.copy(out=u_bf[h][:, :, 0:2], in_=prod_lo[:, :, h * P : (h + 1) * P].rearrange("p t j -> p j t"))
+        nc.vector.tensor_tensor(prod_hi[:, 0, :], xb_sb[2][:].indirect(list_b[:]), scaled[2][:], ALU.mult)
         for h in range(HALVES):
-            nc.vector.tensor_copy(out=u_bf[h][:, :, 2:4], in_=prod_hi[h][:].rearrange("p t j -> p j t"))
+            nc.vector.tensor_tensor(
+                prod_hi[:, 1, h * P : (h + 1) * P],
+                xb_sb[3][:].indirect(list_b[:, h * LIST_COLS : (h + 1) * LIST_COLS]),
+                scaled[3][:, h * P : (h + 1) * P],
+                ALU.mult,
+            )
+        for h in range(HALVES):
+            nc.vector.tensor_copy(out=u_bf[h][:, :, 2:4], in_=prod_hi[:, :, h * P : (h + 1) * P].rearrange("p t j -> p j t"))
         u_q = [sb.tile([P, P], U32, name=f"u_q{h}", align_bytes=64) for h in range(HALVES)]
         u_sc = [sb.tile([P, P], U8, name=f"u_sc{h}", align_bytes=64) for h in range(HALVES)]
-        a_ps = [ps.tile([P, R], F32, name=f"a_ps{h}") for h in range(HALVES)]
+        RH = R // 2
+        a_ps = [[ps.tile([P, RH], F32, name=f"a_ps{h}{g}", tag=f"bank{h}{g}") for g in range(2)] for h in range(HALVES)]
         for h in range(HALVES):
             nc.vector.quantize_mx(out=u_q[h][:].bitcast(E4M3X4), scales=u_sc[h][:], in_=u_bf[h][:].rearrange("p j t -> p (j t)"))
-            nc.tensor.matmul_mx(
-                out=a_ps[h][:], lhsT=u_q[h][:].bitcast(E4M3X4), lhsT_scale=u_sc[h][:],
-                rhs=w_sb[:].bitcast(E2M1X4), rhs_scale=w_sc[:], start=True, stop=True,
-            )
+            for g in range(2):
+                nc.tensor.matmul_mx(
+                    out=a_ps[h][g][:], lhsT=u_q[h][:].bitcast(E4M3X4), lhsT_scale=u_sc[h][:],
+                    rhs=w_sb[:, 2 * RH * g : 2 * RH * (g + 1)].bitcast(E2M1X4), rhs_scale=w_sc[:, RH * g : RH * (g + 1)],
+                    start=True, stop=True,
+                )
 
         pos = [sb.tile([P, 2, P, 2], F32, name=f"pos{h}") for h in range(HALVES)]
-        peak = [sb.tile([P, 1], F32, name=f"peak{h}") for h in range(HALVES)]
+        peak = [[sb.tile([P, 1], F32, name=f"peak{h}{g}") for g in range(2)] for h in range(HALVES)]
         den = [sb.tile([P, 1], F32, name=f"den{h}") for h in range(HALVES)]
         inv = [sb.tile([P, 1], F32, name=f"inv{h}") for h in range(HALVES)]
-        hr = [sb.tile([P, R], BF16, name=f"hr{h}") for h in range(HALVES)]
+        hr = [[sb.tile([P, P, 2], BF16, name=f"hr{h}{u}") for u in range(2)] for h in range(HALVES)]
+        QH = P // 2
         for h in range(HALVES):
+            for g in range(2):
+                nc.vector.tensor_scalar(
+                    out=pos[h][:, :, QH * g : QH * (g + 1), :], in0=a_ps[h][g][:].rearrange("p (q u e) -> p u q e", u=2, e=2),
+                    scalar1=0.0, scalar2=None, op0=ALU.max, op1=ALU.max, accum_out=peak[h][g][:],
+                )
             nc.vector.tensor_scalar(
-                out=pos[h][:], in0=a_ps[h][:].rearrange("p (q u e) -> p u q e", u=2, e=2),
-                scalar1=0.0, scalar2=None, op0=ALU.max, op1=ALU.max, accum_out=peak[h][:],
+                out=den[h][:], in0=peak[h][0][:], scalar1=peak[h][1][:], scalar2=PEAK_SHIFT, op0=ALU.max, op1=ALU.add
             )
-            nc.vector.tensor_scalar(out=den[h][:], in0=peak[h][:], scalar1=PEAK_SHIFT, scalar2=None, op0=ALU.add)
             nc.vector.reciprocal(out=inv[h][:], in_=den[h][:])
-        t_ps = [ps.tile([P, 2, P], F32, name=f"t_ps{h}") for h in range(HALVES)]
+        t_ps = [ps.tile([P, 2, P], F32, name=f"t_ps{h}", tag=f"bank{h}0") for h in range(HALVES)]
         hid_bf = [sb.tile([P, P, PACK], BF16, name=f"hid_bf{h}", align_bytes=64) for h in range(HALVES)]
         for h in range(HALVES):
-            nc.vector.scalar_tensor_tensor(
-                out=hr[h][:], in0=pos[h][:].rearrange("p u q e -> p (u q e)"), scalar=inv[h][:],
-                in1=us_all[:].rearrange("p u q e -> p (u q e)"), op0=ALU.mult, op1=ALU.mult,
-            )
-            words = hr[h][:].bitcast(F32)
             for u in range(2):
-                nc.tensor.transpose(t_ps[h][:, u, :], words[:, u * P : (u + 1) * P], ident[:])
+                nc.vector.scalar_tensor_tensor(
+                    out=hr[h][u][:], in0=pos[h][:, u, :, :], scalar=inv[h][:],
+                    in1=us_all[:, u, :, :], op0=ALU.mult, op1=ALU.mult,
+                )
+                nc.tensor.transpose(t_ps[h][:, u, :], hr[h][u][:].rearrange("p q e -> p (q e)").bitcast(F32), ident[:])
             nc.scalar.copy(out=hid_bf[h][:].bitcast(F32), in_=t_ps[h][:].rearrange("p u j -> p j u"))
 
         hid_q = [sb.tile([P, P], U32, name=f"hid_q{h}", align_bytes=64) for h in range(HALVES)]
         hid_sc = [sb.tile([P, P], U8, name=f"hid_sc{h}", align_bytes=64) for h in range(HALVES)]
         p_ps = [ps.tile([P, N // P, P], F32, name=f"p_ps{h}") for h in range(HALVES)]
-        res = [sb.tile([P, N // P, P], F32, name=f"res{h}") for h in range(HALVES)]
+        res = [[sb.tile([P, P], F32, name=f"res{h}{c}") for c in range(N // P)] for h in range(HALVES)]
         out_rows = out.rearrange("(c p) j -> p c j", p=P)
         for h in range(HALVES):
             nc.vector.quantize_mx(out=hid_q[h][:].bitcast(E5M2X4), scales=hid_sc[h][:], in_=hid_bf[h][:].rearrange("p j t -> p (j t)"))
@@ -154,7 +167,8 @@ def tile_list_rows_entryproducts_peak_residual_kernel(
         for h in range(HALVES):
             for c in range(N // P):
                 nc.vector.scalar_tensor_tensor(
-                    out=res[h][:, c, :], in0=p_ps[h][:, c, :], scalar=gm_sb[:, c : c + 1],
+                    out=res[h][c][:], in0=p_ps[h][:, c, :], scalar=gm_sb[:, c : c + 1],
                     in1=rs_sb[:, c, h * P : (h + 1) * P], op0=ALU.mult, op1=ALU.add,
                 )
-            nc.sync.dma_start(out=out_rows[:, :, h * P : (h + 1) * P], in_=res[h][:])
+                queue = nc.sync if c == 0 else nc.scalar
+                queue.dma_start(out=out_rows[:, c, h * P : (h + 1) * P], in_=res[h][c][:])

@@ -40,11 +40,12 @@ def tile_list_rows_entryproducts_peak_residual_kernel(
 
         list_a = lists.tile([P, J // 16], U16, name="list_a")
         list_b = lists.tile([P, J // 16], U16, name="list_b")
-        xa_rows = xa.rearrange("(p t) c -> t p c", t=PACK)
+        xa_rows = xa.rearrange("(p t) c -> p t c", t=PACK)
         xb_rows = xb.rearrange("(p t) c -> t p c", t=PACK)
-        xa_lo = [sb.tile([P, T], F32, name=f"xa{t}") for t in range(2)]
-        xa_hi = sb.tile([P, 2, T], F32, name="xa_hi")
-        xa_sb = [xa_lo[0][:], xa_lo[1][:], xa_hi[:, 0, :], xa_hi[:, 1, :]]
+        xa_first = sb.tile([P, T], F32, name="xa_first")
+        xa_mid = sb.tile([P, 2, T], F32, name="xa_mid")
+        xa_last = sb.tile([P, T], F32, name="xa_last")
+        xa_sb = [xa_first[:], xa_mid[:, 0, :], xa_mid[:, 1, :], xa_last[:]]
         xb_sb = [sb.tile([P, S], F32, name=f"xb{t}") for t in range(PACK)]
         fk_sb = sb.tile([P, PACK], F32, name="fk_sb")
         us_sb = sb.tile([P, PACK], F32, name="us_sb")
@@ -56,17 +57,17 @@ def tile_list_rows_entryproducts_peak_residual_kernel(
         wb_sc = sb.tile([P, N], U8, name="wb_sc", align_bytes=64)
 
         nc.sync.dma_start(list_a[:], offs)
-        nc.sync.dma_start(out=xa_sb[0], in_=xa_rows[0])
+        nc.scalar.dma_start(out=xa_first[:], in_=xa_rows[:, 0, :])
         nc.sync.dma_start(out=fk_sb[:], in_=fk.rearrange("(p t) o -> p (t o)", t=PACK))
-        nc.sync.dma_start(out=xa_sb[1], in_=xa_rows[1])
-        nc.sync.dma_start(out=xa_hi[:], in_=xa.rearrange("(p t) c -> p t c", t=PACK)[:, 2:4, :])
+        nc.sync.dma_start(out=xa_mid[:], in_=xa_rows[:, 1:3, :])
         nc.sync.dma_start(list_b[:], offs2)
         nc.sync.dma_start(out=xb_sb[0][:], in_=xb_rows[0])
-        nc.sync.dma_start(out=us_sb[:], in_=us.rearrange("o (p t) -> p (o t)", t=PACK))
+        nc.sync.dma_start(out=xa_last[:], in_=xa_rows[:, 3, :])
         for t in range(1, PACK):
             nc.sync.dma_start(out=xb_sb[t][:], in_=xb_rows[t])
         nc.sync.dma_start(out=w_sb[:].bitcast(I32), in_=w_words[0].bitcast(I32))
         load_scale_rows(nc.sync, w_sc, w_scales)
+        nc.sync.dma_start(out=us_sb[:], in_=us.rearrange("o (p t) -> p (o t)", t=PACK))
         load_scale_rows(nc.sync, wb_sc, wb_scales)
         nc.sync.dma_start(out=wb_sb[:].bitcast(I32), in_=wb_words[0].rearrange("p n t -> p (n t)").bitcast(I32))
         nc.sync.dma_start(out=rs_sb[:], in_=rs.rearrange("(c p) j -> p c j", p=P))
@@ -80,10 +81,6 @@ def tile_list_rows_entryproducts_peak_residual_kernel(
         nc.scalar.activation(out=distance[:], in_=offset[:], func=ACT.Abs)
         nc.scalar.activation(out=ident[:], in_=distance[:], func=ACT.Relu, scale=-1.0, bias=1.0)
 
-        us_all = ps.tile([P, 2, P, 2], F32, name="us_all")
-        for t in range(PACK):
-            nc.tensor.transpose(us_all[:, t // 2, :, t % 2], us_sb[:, t : t + 1].to_broadcast([P, P]), ident[:])
-
         picked_lo = sb.tile([P, 2, J], F32, name="picked_lo", tag="picked_lo")
         picked_hi = sb.tile([P, 2, J], F32, name="picked_hi", tag="picked_hi")
         picked = [picked_lo[:, 0, :], picked_lo[:, 1, :], picked_hi[:, 0, :], picked_hi[:, 1, :]]
@@ -96,7 +93,7 @@ def tile_list_rows_entryproducts_peak_residual_kernel(
             nc.scalar.activation(out=scaled[t][:], in_=picked[t], func=ACT.Copy, scale=fk_sb[:, t : t + 1])
 
         u_bf = [sb.tile([P, P, PACK], BF16, name=f"u_bf{h}", align_bytes=64) for h in range(HALVES)]
-        prod_lo = sb.tile([P, 2, J], F32, name="prod_lo", tag="picked_lo")
+        prod_lo = sb.tile([P, 2, J], F32, name="prod_lo")
         prod_hi = sb.tile([P, 2, J], F32, name="prod_hi")
         for t in range(2):
             nc.vector.tensor_tensor(prod_lo[:, t, :], xb_sb[t][:].indirect(list_b[:]), scaled[t][:], ALU.mult)
@@ -141,34 +138,40 @@ def tile_list_rows_entryproducts_peak_residual_kernel(
                 out=den[h][:], in0=peak[h][0][:], scalar1=peak[h][1][:], scalar2=PEAK_SHIFT, op0=ALU.max, op1=ALU.add
             )
             nc.vector.reciprocal(out=inv[h][:], in_=den[h][:])
-        t_ps = [ps.tile([P, 2, P], F32, name=f"t_ps{h}", tag=f"bank{h}0") for h in range(HALVES)]
-        hid_bf = [sb.tile([P, P, PACK], BF16, name=f"hid_bf{h}", align_bytes=64) for h in range(HALVES)]
+        us_all = [ps.tile([P, P, 2], F32, name=f"us_all{u}", tag=f"bank0{u}") for u in range(2)]
+        for t in range(PACK):
+            nc.tensor.transpose(us_all[t // 2][:, :, t % 2], us_sb[:, t : t + 1].to_broadcast([P, P]), ident[:])
+        t_ps = [ps.tile([P, 2, P], F32, name=f"t_ps{h}", tag=f"bank1{h}") for h in range(HALVES)]
+        hid_bf = [sb.tile([P, P, PACK], BF16, name=f"hid_bf{h}", tag=f"hid_bf{h}", align_bytes=64) for h in range(HALVES)]
         for h in range(HALVES):
             for u in range(2):
                 nc.vector.scalar_tensor_tensor(
                     out=hr[h][u][:], in0=pos[h][:, u, :, :], scalar=inv[h][:],
-                    in1=us_all[:, u, :, :], op0=ALU.mult, op1=ALU.mult,
+                    in1=us_all[u][:], op0=ALU.mult, op1=ALU.mult,
                 )
                 nc.tensor.transpose(t_ps[h][:, u, :], hr[h][u][:].rearrange("p q e -> p (q e)").bitcast(F32), ident[:])
             nc.scalar.copy(out=hid_bf[h][:].bitcast(F32), in_=t_ps[h][:].rearrange("p u j -> p j u"))
 
         hid_q = [sb.tile([P, P], U32, name=f"hid_q{h}", align_bytes=64) for h in range(HALVES)]
         hid_sc = [sb.tile([P, P], U8, name=f"hid_sc{h}", align_bytes=64) for h in range(HALVES)]
-        p_ps = [ps.tile([P, N // P, P], F32, name=f"p_ps{h}") for h in range(HALVES)]
-        res = [[sb.tile([P, P], F32, name=f"res{h}{c}") for c in range(N // P)] for h in range(HALVES)]
+        p_ps = [[ps.tile([P, P], F32, name=f"p_ps{h}{c}") for c in range(N // P)] for h in range(HALVES)]
+        res_first = sb.tile([P, N // P, P], F32, name="res_first", tag="hid_bf1", align_bytes=64)
+        res_last = [sb.tile([P, P], F32, name=f"res_last{c}") for c in range(N // P)]
+        res = [[res_first[:, c, :] for c in range(N // P)], [res_last[c][:] for c in range(N // P)]]
         out_rows = out.rearrange("(c p) j -> p c j", p=P)
         for h in range(HALVES):
             nc.vector.quantize_mx(out=hid_q[h][:].bitcast(E5M2X4), scales=hid_sc[h][:], in_=hid_bf[h][:].rearrange("p j t -> p (j t)"))
             for c in range(N // P):
                 nc.tensor.matmul_mx(
-                    out=p_ps[h][:, c, :], lhsT=wb_sb[:, c * P : (c + 1) * P].bitcast(E4M3X4), lhsT_scale=wb_sc[:, c * P : (c + 1) * P],
+                    out=p_ps[h][c][:], lhsT=wb_sb[:, c * P : (c + 1) * P].bitcast(E4M3X4), lhsT_scale=wb_sc[:, c * P : (c + 1) * P],
                     rhs=hid_q[h][:].bitcast(E5M2X4), rhs_scale=hid_sc[h][:], start=True, stop=True,
                 )
         for h in range(HALVES):
             for c in range(N // P):
                 nc.vector.scalar_tensor_tensor(
-                    out=res[h][c][:], in0=p_ps[h][:, c, :], scalar=gm_sb[:, c : c + 1],
+                    out=res[h][c], in0=p_ps[h][c][:], scalar=gm_sb[:, c : c + 1],
                     in1=rs_sb[:, c, h * P : (h + 1) * P], op0=ALU.mult, op1=ALU.add,
                 )
-                queue = nc.sync if c == 0 else nc.scalar
-                queue.dma_start(out=out_rows[:, c, h * P : (h + 1) * P], in_=res[h][c][:])
+        nc.sync.dma_start(out=out_rows[:, :, 0:P], in_=res_first[:])
+        nc.sync.dma_start(out=out_rows[:, 0, P:J], in_=res[1][0])
+        nc.scalar.dma_start(out=out_rows[:, 1, P:J], in_=res[1][1])

@@ -21,11 +21,13 @@ P = 128
 PACK = 4
 HALVES = J // P
 LIST_COLS = P // 16
+R_PART = R // 2
+N_TILES = N // P
 PEAK_SHIFT = 0.3
 
 
-def load_scale_rows(queue, plane, scales):
-    for q in range(4):
+def load_scale_rows(queue, plane, scales, quadrants):
+    for q in quadrants:
         queue.dma_start(out=plane[32 * q : 32 * q + 4, :].bitcast(I32), in_=scales[0, 4 * q : 4 * q + 4, :].bitcast(I32))
 
 
@@ -49,8 +51,8 @@ def tile_list_rows_entryproducts_peak_residual_kernel(
         xb_sb = [sb.tile([P, S], F32, name=f"xb{t}") for t in range(PACK)]
         fk_sb = sb.tile([P, PACK], F32, name="fk_sb")
         us_sb = sb.tile([P, PACK], F32, name="us_sb")
-        gm_sb = sb.tile([P, N // P], F32, name="gm_sb")
-        rs_sb = sb.tile([P, N // P, J], F32, name="rs_sb")
+        gm_sb = sb.tile([P, N_TILES], F32, name="gm_sb")
+        rs_sb = sb.tile([P, N_TILES, J], F32, name="rs_sb")
         w_sb = sb.tile([P, 2 * R], U8, name="w_sb", align_bytes=64)
         w_sc = sb.tile([P, R], U8, name="w_sc", align_bytes=64)
         wb_sb = sb.tile([P, N], U32, name="wb_sb", align_bytes=64)
@@ -65,21 +67,26 @@ def tile_list_rows_entryproducts_peak_residual_kernel(
         nc.sync.dma_start(out=xa_last[:], in_=xa_rows[:, 3, :])
         for t in range(1, PACK):
             nc.sync.dma_start(out=xb_sb[t][:], in_=xb_rows[t])
-        nc.sync.dma_start(out=w_sb[:].bitcast(I32), in_=w_words[0].bitcast(I32))
-        load_scale_rows(nc.sync, w_sc, w_scales)
         nc.sync.dma_start(out=us_sb[:], in_=us.rearrange("o (p t) -> p (o t)", t=PACK))
-        load_scale_rows(nc.sync, wb_sc, wb_scales)
+        nc.sync.dma_start(out=w_sb[:].bitcast(I32), in_=w_words[0].bitcast(I32))
+        load_scale_rows(nc.sync, w_sc, w_scales, range(2))
+        load_scale_rows(nc.sync, wb_sc, wb_scales, range(4))
         nc.sync.dma_start(out=wb_sb[:].bitcast(I32), in_=wb_words[0].rearrange("p n t -> p (n t)").bitcast(I32))
         nc.sync.dma_start(out=rs_sb[:], in_=rs.rearrange("(c p) j -> p c j", p=P))
-        with nc.allow_non_contiguous_dma(reason="one factor a partition"):
+        with nc.allow_non_contiguous_dma(reason="one factor a partition and tile of output features"):
             nc.sync.dma_start(out=gm_sb[:], in_=gm.rearrange("(c p) o -> p (c o)", p=P))
 
         ident = sb.tile([P, P], F32, name="ident")
         offset = sb.tile([P, P], F32, name="offset", tag="picked_lo")
         distance = sb.tile([P, P], F32, name="distance", tag="picked_hi")
         nc.gpsimd.iota(offset[:], pattern=[[1, P]], base=0, channel_multiplier=-1, allow_small_or_imprecise_dtypes=True)
+        load_scale_rows(nc.gpsimd, w_sc, w_scales, range(2, 4))
         nc.scalar.activation(out=distance[:], in_=offset[:], func=ACT.Abs)
         nc.scalar.activation(out=ident[:], in_=distance[:], func=ACT.Relu, scale=-1.0, bias=1.0)
+
+        us_all = ps.tile([P, 2, P, 2], F32, name="us_all")
+        for t in range(PACK):
+            nc.tensor.transpose(us_all[:, t // 2, :, t % 2], us_sb[:, t : t + 1].to_broadcast([P, P]), ident[:])
 
         picked_lo = sb.tile([P, 2, J], F32, name="picked_lo", tag="picked_lo")
         picked_hi = sb.tile([P, 2, J], F32, name="picked_hi", tag="picked_hi")
@@ -109,17 +116,21 @@ def tile_list_rows_entryproducts_peak_residual_kernel(
             )
         for h in range(HALVES):
             nc.vector.tensor_copy(out=u_bf[h][:, :, 2:4], in_=prod_hi[:, :, h * P : (h + 1) * P].rearrange("p t j -> p j t"))
+
         u_q = [sb.tile([P, P], U32, name=f"u_q{h}", align_bytes=64) for h in range(HALVES)]
         u_sc = [sb.tile([P, P], U8, name=f"u_sc{h}", align_bytes=64) for h in range(HALVES)]
-        RH = R // 2
-        a_ps = [[ps.tile([P, RH], F32, name=f"a_ps{h}{g}", tag=f"bank{h}{g}") for g in range(2)] for h in range(HALVES)]
+        a_ps = [[ps.tile([P, R_PART], F32, name=f"a_ps{h}{g}", tag=f"bank{h}{g}") for g in range(2)] for h in range(HALVES)]
         for h in range(HALVES):
             nc.vector.quantize_mx(out=u_q[h][:].bitcast(E4M3X4), scales=u_sc[h][:], in_=u_bf[h][:].rearrange("p j t -> p (j t)"))
             for g in range(2):
                 nc.tensor.matmul_mx(
-                    out=a_ps[h][g][:], lhsT=u_q[h][:].bitcast(E4M3X4), lhsT_scale=u_sc[h][:],
-                    rhs=w_sb[:, 2 * RH * g : 2 * RH * (g + 1)].bitcast(E2M1X4), rhs_scale=w_sc[:, RH * g : RH * (g + 1)],
-                    start=True, stop=True,
+                    out=a_ps[h][g][:],
+                    lhsT=u_q[h][:].bitcast(E4M3X4),
+                    lhsT_scale=u_sc[h][:],
+                    rhs=w_sb[:, 2 * R_PART * g : 2 * R_PART * (g + 1)].bitcast(E2M1X4),
+                    rhs_scale=w_sc[:, R_PART * g : R_PART * (g + 1)],
+                    start=True,
+                    stop=True,
                 )
 
         pos = [sb.tile([P, 2, P, 2], F32, name=f"pos{h}") for h in range(HALVES)]
@@ -127,50 +138,69 @@ def tile_list_rows_entryproducts_peak_residual_kernel(
         den = [sb.tile([P, 1], F32, name=f"den{h}") for h in range(HALVES)]
         inv = [sb.tile([P, 1], F32, name=f"inv{h}") for h in range(HALVES)]
         hr = [[sb.tile([P, P, 2], BF16, name=f"hr{h}{u}") for u in range(2)] for h in range(HALVES)]
-        QH = P // 2
+        q_part = R_PART // PACK
         for h in range(HALVES):
             for g in range(2):
                 nc.vector.tensor_scalar(
-                    out=pos[h][:, :, QH * g : QH * (g + 1), :], in0=a_ps[h][g][:].rearrange("p (q u e) -> p u q e", u=2, e=2),
-                    scalar1=0.0, scalar2=None, op0=ALU.max, op1=ALU.max, accum_out=peak[h][g][:],
+                    out=pos[h][:, :, q_part * g : q_part * (g + 1), :],
+                    in0=a_ps[h][g][:].rearrange("p (q u e) -> p u q e", u=2, e=2),
+                    scalar1=0.0,
+                    scalar2=None,
+                    op0=ALU.max,
+                    op1=ALU.max,
+                    accum_out=peak[h][g][:],
                 )
             nc.vector.tensor_scalar(
                 out=den[h][:], in0=peak[h][0][:], scalar1=peak[h][1][:], scalar2=PEAK_SHIFT, op0=ALU.max, op1=ALU.add
             )
             nc.vector.reciprocal(out=inv[h][:], in_=den[h][:])
-        us_all = [ps.tile([P, P, 2], F32, name=f"us_all{u}", tag=f"bank0{u}") for u in range(2)]
-        for t in range(PACK):
-            nc.tensor.transpose(us_all[t // 2][:, :, t % 2], us_sb[:, t : t + 1].to_broadcast([P, P]), ident[:])
-        t_ps = [ps.tile([P, 2, P], F32, name=f"t_ps{h}", tag=f"bank1{h}") for h in range(HALVES)]
+
+        t_ps = [ps.tile([P, 2, P], F32, name=f"t_ps{h}", tag=f"bank0{h}") for h in range(HALVES)]
         hid_bf = [sb.tile([P, P, PACK], BF16, name=f"hid_bf{h}", tag=f"hid_bf{h}", align_bytes=64) for h in range(HALVES)]
         for h in range(HALVES):
             for u in range(2):
                 nc.vector.scalar_tensor_tensor(
-                    out=hr[h][u][:], in0=pos[h][:, u, :, :], scalar=inv[h][:],
-                    in1=us_all[u][:], op0=ALU.mult, op1=ALU.mult,
+                    out=hr[h][u][:],
+                    in0=pos[h][:, u, :, :],
+                    scalar=inv[h][:],
+                    in1=us_all[:, u, :, :],
+                    op0=ALU.mult,
+                    op1=ALU.mult,
                 )
                 nc.tensor.transpose(t_ps[h][:, u, :], hr[h][u][:].rearrange("p q e -> p (q e)").bitcast(F32), ident[:])
             nc.scalar.copy(out=hid_bf[h][:].bitcast(F32), in_=t_ps[h][:].rearrange("p u j -> p j u"))
 
         hid_q = [sb.tile([P, P], U32, name=f"hid_q{h}", align_bytes=64) for h in range(HALVES)]
         hid_sc = [sb.tile([P, P], U8, name=f"hid_sc{h}", align_bytes=64) for h in range(HALVES)]
-        p_ps = [[ps.tile([P, P], F32, name=f"p_ps{h}{c}") for c in range(N // P)] for h in range(HALVES)]
-        res_first = sb.tile([P, N // P, P], F32, name="res_first", tag="hid_bf1", align_bytes=64)
-        res_last = [sb.tile([P, P], F32, name=f"res_last{c}") for c in range(N // P)]
-        res = [[res_first[:, c, :] for c in range(N // P)], [res_last[c][:] for c in range(N // P)]]
+        p_ps = [
+            [ps.tile([P, P], F32, name=f"p_ps{h}{c}", tag=(f"bank1{c}" if h == 0 else f"out{c}")) for c in range(N_TILES)]
+            for h in range(HALVES)
+        ]
+        res_first = sb.tile([P, N_TILES, P], F32, name="res_first", tag="hid_bf1", align_bytes=64)
+        res_last = [sb.tile([P, P], F32, name=f"res_last{c}") for c in range(N_TILES)]
+        res = [[res_first[:, c, :] for c in range(N_TILES)], [res_last[c][:] for c in range(N_TILES)]]
         out_rows = out.rearrange("(c p) j -> p c j", p=P)
         for h in range(HALVES):
             nc.vector.quantize_mx(out=hid_q[h][:].bitcast(E5M2X4), scales=hid_sc[h][:], in_=hid_bf[h][:].rearrange("p j t -> p (j t)"))
-            for c in range(N // P):
+            for c in range(N_TILES):
                 nc.tensor.matmul_mx(
-                    out=p_ps[h][c][:], lhsT=wb_sb[:, c * P : (c + 1) * P].bitcast(E4M3X4), lhsT_scale=wb_sc[:, c * P : (c + 1) * P],
-                    rhs=hid_q[h][:].bitcast(E5M2X4), rhs_scale=hid_sc[h][:], start=True, stop=True,
+                    out=p_ps[h][c][:],
+                    lhsT=wb_sb[:, c * P : (c + 1) * P].bitcast(E4M3X4),
+                    lhsT_scale=wb_sc[:, c * P : (c + 1) * P],
+                    rhs=hid_q[h][:].bitcast(E5M2X4),
+                    rhs_scale=hid_sc[h][:],
+                    start=True,
+                    stop=True,
                 )
         for h in range(HALVES):
-            for c in range(N // P):
+            for c in range(N_TILES):
                 nc.vector.scalar_tensor_tensor(
-                    out=res[h][c], in0=p_ps[h][c][:], scalar=gm_sb[:, c : c + 1],
-                    in1=rs_sb[:, c, h * P : (h + 1) * P], op0=ALU.mult, op1=ALU.add,
+                    out=res[h][c],
+                    in0=p_ps[h][c][:],
+                    scalar=gm_sb[:, c : c + 1],
+                    in1=rs_sb[:, c, h * P : (h + 1) * P],
+                    op0=ALU.mult,
+                    op1=ALU.add,
                 )
         nc.sync.dma_start(out=out_rows[:, :, 0:P], in_=res_first[:])
         nc.sync.dma_start(out=out_rows[:, 0, P:J], in_=res[1][0])

from contextlib import ExitStack

import concourse.mybir as mybir

K, T, J, S, R, N = 512, 512, 256, 512, 512, 256
FLOPS = 2 * K * J * R + 2 * R * N * J

F32 = mybir.dt.float32
BF16 = mybir.dt.bfloat16
I32 = mybir.dt.int32
U32 = mybir.dt.uint32
U16 = mybir.dt.uint16
U8 = mybir.dt.uint8
E4M3X4 = mybir.dt.float8_e4m3fn_x4
E5M2X4 = mybir.dt.float8_e5m2_x4
E2M1X4 = mybir.dt.float4_e2m1fn_x4
ALU = mybir.AluOpType
ACT = mybir.ActivationFunctionType

P = 128
PACK = 4
HALVES = J // P
LIST_COLS = P // 16
R_PART = R // 2
N_TILES = N // P
PEAK_SHIFT = 0.3


def load_scale_rows(queue, plane, scales, quadrants):
    for q in quadrants:
        queue.dma_start(out=plane[32 * q : 32 * q + 4, :].bitcast(I32), in_=scales[0, 4 * q : 4 * q + 4, :].bitcast(I32))


def tile_list_rows_entryproducts_peak_residual_kernel(
    tc, xa, xb, fk, w_words, w_scales, us, wb_words, wb_scales, rs, gm, offs, offs2, out
):
    nc = tc.nc
    with ExitStack() as ctx:
        lists = ctx.enter_context(tc.tile_pool(name="lists", bufs=1))
        sb = ctx.enter_context(tc.tile_pool(name="sb", bufs=1))
        ps = ctx.enter_context(tc.psum_pool(name="ps", bufs=1))

        list_a = lists.tile([P, J // 16], U16, name="list_a")
        list_b = lists.tile([P, J // 16], U16, name="list_b")
        xa_rows = xa.rearrange("(p t) c -> p t c", t=PACK)
        xb_rows = xb.rearrange("(p t) c -> t p c", t=PACK)
        xa_first = sb.tile([P, T], F32, name="xa_first")
        xa_mid = sb.tile([P, 2, T], F32, name="xa_mid")
        xa_last = sb.tile([P, T], F32, name="xa_last")
        xa_sb = [xa_first[:], xa_mid[:, 0, :], xa_mid[:, 1, :], xa_last[:]]
        xb_sb = [sb.tile([P, S], F32, name=f"xb{t}") for t in range(PACK)]
        fk_sb = sb.tile([P, PACK], F32, name="fk_sb")
        us_sb = sb.tile([P, PACK], F32, name="us_sb")
        gm_sb = sb.tile([P, N_TILES], F32, name="gm_sb")
        rs_sb = sb.tile([P, N_TILES, J], F32, name="rs_sb")
        w_sb = sb.tile([P, 2 * R], U8, name="w_sb", align_bytes=64)
        w_sc = sb.tile([P, R], U8, name="w_sc", align_bytes=64)
        wb_sb = sb.tile([P, N], U32, name="wb_sb", align_bytes=64)
        wb_sc = sb.tile([P, N], U8, name="wb_sc", align_bytes=64)

        nc.sync.dma_start(list_a[:], offs)
        nc.scalar.dma_start(out=xa_first[:], in_=xa_rows[:, 0, :])
        nc.sync.dma_start(out=fk_sb[:], in_=fk.rearrange("(p t) o -> p (t o)", t=PACK))
        nc.sync.dma_start(out=xa_mid[:], in_=xa_rows[:, 1:3, :])
        nc.sync.dma_start(list_b[:], offs2)
        nc.sync.dma_start(out=xb_sb[0][:], in_=xb_rows[0])
        nc.sync.dma_start(out=xa_last[:], in_=xa_rows[:, 3, :])
        for t in range(1, PACK):
            nc.sync.dma_start(out=xb_sb[t][:], in_=xb_rows[t])
        nc.sync.dma_start(out=us_sb[:], in_=us.rearrange("o (p t) -> p (o t)", t=PACK))
        nc.sync.dma_start(out=w_sb[:].bitcast(I32), in_=w_words[0].bitcast(I32))
        load_scale_rows(nc.sync, w_sc, w_scales, range(2))
        load_scale_rows(nc.sync, wb_sc, wb_scales, range(4))
        nc.sync.dma_start(out=wb_sb[:].bitcast(I32), in_=wb_words[0].rearrange("p n t -> p (n t)").bitcast(I32))
        nc.sync.dma_start(out=rs_sb[:], in_=rs.rearrange("(c p) j -> p c j", p=P))
        with nc.allow_non_contiguous_dma(reason="one factor a partition and tile of output features"):
            nc.sync.dma_start(out=gm_sb[:], in_=gm.rearrange("(c p) o -> p (c o)", p=P))

        ident = sb.tile([P, P], F32, name="ident")
        offset = sb.tile([P, P], F32, name="offset", tag="picked_lo")
        distance = sb.tile([P, P], F32, name="distance", tag="picked_hi")
        nc.gpsimd.iota(offset[:], pattern=[[1, P]], base=0, channel_multiplier=-1, allow_small_or_imprecise_dtypes=True)
        load_scale_rows(nc.gpsimd, w_sc, w_scales, range(2, 4))
        nc.scalar.activation(out=distance[:], in_=offset[:], func=ACT.Abs)
        nc.scalar.activation(out=ident[:], in_=distance[:], func=ACT.Relu, scale=-1.0, bias=1.0)

        us_all = ps.tile([P, 2, P, 2], F32, name="us_all")
        for t in range(PACK):
            nc.tensor.transpose(us_all[:, t // 2, :, t % 2], us_sb[:, t : t + 1].to_broadcast([P, P]), ident[:])

        picked_lo = sb.tile([P, 2, J], F32, name="picked_lo", tag="picked_lo")
        picked_hi = sb.tile([P, 2, J], F32, name="picked_hi", tag="picked_hi")
        picked = [picked_lo[:, 0, :], picked_lo[:, 1, :], picked_hi[:, 0, :], picked_hi[:, 1, :]]
        scaled = [sb.tile([P, J], F32, name=f"scaled{t}") for t in range(PACK)]
        for t in range(PACK):
            nc.scalar.activation(out=picked[t], in_=xa_sb[t].indirect(list_a[:]), func=ACT.Copy)
        for t in range(2):
            nc.vector.tensor_scalar(out=scaled[t][:], in0=picked[t], scalar1=fk_sb[:, t : t + 1], scalar2=None, op0=ALU.mult)
        for t in range(2, PACK):
            nc.scalar.activation(out=scaled[t][:], in_=picked[t], func=ACT.Copy, scale=fk_sb[:, t : t + 1])

        u_bf = [sb.tile([P, P, PACK], BF16, name=f"u_bf{h}", align_bytes=64) for h in range(HALVES)]
        prod_lo = sb.tile([P, 2, J], F32, name="prod_lo")
        prod_hi = sb.tile([P, 2, J], F32, name="prod_hi")
        for t in range(2):
            nc.vector.tensor_tensor(prod_lo[:, t, :], xb_sb[t][:].indirect(list_b[:]), scaled[t][:], ALU.mult)
        for h in range(HALVES):
            nc.scalar.copy(out=u_bf[h][:, :, 0:2], in_=prod_lo[:, :, h * P : (h + 1) * P].rearrange("p t j -> p j t"))
        nc.vector.tensor_tensor(prod_hi[:, 0, :], xb_sb[2][:].indirect(list_b[:]), scaled[2][:], ALU.mult)
        for h in range(HALVES):
            nc.vector.tensor_tensor(
                prod_hi[:, 1, h * P : (h + 1) * P],
                xb_sb[3][:].indirect(list_b[:, h * LIST_COLS : (h + 1) * LIST_COLS]),
                scaled[3][:, h * P : (h + 1) * P],
                ALU.mult,
            )
        for h in range(HALVES):
            nc.vector.tensor_copy(out=u_bf[h][:, :, 2:4], in_=prod_hi[:, :, h * P : (h + 1) * P].rearrange("p t j -> p j t"))

        u_q = [sb.tile([P, P], U32, name=f"u_q{h}", align_bytes=64) for h in range(HALVES)]
        u_sc = [sb.tile([P, P], U8, name=f"u_sc{h}", align_bytes=64) for h in range(HALVES)]
        a_ps = [[ps.tile([P, R_PART], F32, name=f"a_ps{h}{g}", tag=f"bank{h}{g}") for g in range(2)] for h in range(HALVES)]
        for h in range(HALVES):
            nc.vector.quantize_mx(out=u_q[h][:].bitcast(E4M3X4), scales=u_sc[h][:], in_=u_bf[h][:].rearrange("p j t -> p (j t)"))
            for g in range(2):
                nc.tensor.matmul_mx(
                    out=a_ps[h][g][:],
                    lhsT=u_q[h][:].bitcast(E4M3X4),
                    lhsT_scale=u_sc[h][:],
                    rhs=w_sb[:, 2 * R_PART * g : 2 * R_PART * (g + 1)].bitcast(E2M1X4),
                    rhs_scale=w_sc[:, R_PART * g : R_PART * (g + 1)],
                    start=True,
                    stop=True,
                )

        pos = [sb.tile([P, 2, P, 2], F32, name=f"pos{h}") for h in range(HALVES)]
        peak = [[sb.tile([P, 1], F32, name=f"peak{h}{g}") for g in range(2)] for h in range(HALVES)]
        den = [sb.tile([P, 1], F32, name=f"den{h}") for h in range(HALVES)]
        inv = [sb.tile([P, 1], F32, name=f"inv{h}") for h in range(HALVES)]
        hr = [[sb.tile([P, P, 2], BF16, name=f"hr{h}{u}") for u in range(2)] for h in range(HALVES)]
        q_part = R_PART // PACK
        for h in range(HALVES):
            for g in range(2):
                nc.vector.tensor_scalar(
                    out=pos[h][:, :, q_part * g : q_part * (g + 1), :],
                    in0=a_ps[h][g][:].rearrange("p (q u e) -> p u q e", u=2, e=2),
                    scalar1=0.0,
                    scalar2=None,
                    op0=ALU.max,
                    op1=ALU.max,
                    accum_out=peak[h][g][:],
                )
            nc.vector.tensor_scalar(
                out=den[h][:], in0=peak[h][0][:], scalar1=peak[h][1][:], scalar2=PEAK_SHIFT, op0=ALU.max, op1=ALU.add
            )
            nc.vector.reciprocal(out=inv[h][:], in_=den[h][:])

        t_ps = [ps.tile([P, 2, P], F32, name=f"t_ps{h}", tag=f"bank0{h}") for h in range(HALVES)]
        hid_bf = [sb.tile([P, P, PACK], BF16, name=f"hid_bf{h}", tag=f"hid_bf{h}", align_bytes=64) for h in range(HALVES)]
        for h in range(HALVES):
            for u in range(2):
                nc.vector.scalar_tensor_tensor(
                    out=hr[h][u][:],
                    in0=pos[h][:, u, :, :],
                    scalar=inv[h][:],
                    in1=us_all[:, u, :, :],
                    op0=ALU.mult,
                    op1=ALU.mult,
                )
                nc.tensor.transpose(t_ps[h][:, u, :], hr[h][u][:].rearrange("p q e -> p (q e)").bitcast(F32), ident[:])
            nc.scalar.copy(out=hid_bf[h][:].bitcast(F32), in_=t_ps[h][:].rearrange("p u j -> p j u"))

        hid_q = [sb.tile([P, P], U32, name=f"hid_q{h}", align_bytes=64) for h in range(HALVES)]
        hid_sc = [sb.tile([P, P], U8, name=f"hid_sc{h}", align_bytes=64) for h in range(HALVES)]
        p_ps = [
            [ps.tile([P, P], F32, name=f"p_ps{h}{c}", tag=(f"bank1{c}" if h == 0 else f"out{c}")) for c in range(N_TILES)]
            for h in range(HALVES)
        ]
        res_first = sb.tile([P, N_TILES, P], F32, name="res_first", tag="hid_bf1", align_bytes=64)
        res_last = [sb.tile([P, P], F32, name=f"res_last{c}") for c in range(N_TILES)]
        res = [[res_first[:, c, :] for c in range(N_TILES)], [res_last[c][:] for c in range(N_TILES)]]
        out_rows = out.rearrange("(c p) j -> p c j", p=P)
        for h in range(HALVES):
            nc.vector.quantize_mx(out=hid_q[h][:].bitcast(E5M2X4), scales=hid_sc[h][:], in_=hid_bf[h][:].rearrange("p j t -> p (j t)"))
            for c in range(N_TILES):
                nc.tensor.matmul_mx(
                    out=p_ps[h][c][:],
                    lhsT=wb_sb[:, c * P : (c + 1) * P].bitcast(E4M3X4),
                    lhsT_scale=wb_sc[:, c * P : (c + 1) * P],
                    rhs=hid_q[h][:].bitcast(E5M2X4),
                    rhs_scale=hid_sc[h][:],
                    start=True,
                    stop=True,
                )
        for h in range(HALVES):
            for c in range(N_TILES):
                nc.vector.scalar_tensor_tensor(
                    out=res[h][c],
                    in0=p_ps[h][c][:],
                    scalar=gm_sb[:, c : c + 1],
                    in1=rs_sb[:, c, h * P : (h + 1) * P],
                    op0=ALU.mult,
                    op1=ALU.add,
                )
        nc.sync.dma_start(out=out_rows[:, :, 0:P], in_=res_first[:])
        nc.sync.dma_start(out=out_rows[:, 0, P:J], in_=res[1][0])
        nc.scalar.dma_start(out=out_rows[:, 1, P:J], in_=res[1][1])
